import numpy as np
import ml_dtypes


def mxq(x, axis, fmt="e4m3"):
    dtype, down = {"e4m3": (ml_dtypes.float8_e4m3fn, 7), "e5m2": (ml_dtypes.float8_e5m2, 14)}[fmt]
    v = np.moveaxis(np.asarray(x, np.float32).astype(ml_dtypes.bfloat16).astype(np.float64), axis, -1)
    blocks = v.reshape(v.shape[:-1] + (-1, 32))
    amax = np.abs(blocks).max(-1, keepdims=True)
    byte = np.maximum(np.where(amax > 0, np.frexp(amax)[1] - 1 + 127, 0) - down, 1)
    scale = np.exp2(byte - 127.0)
    codes = (blocks / scale).astype(np.float32).astype(dtype).astype(np.float64)
    return np.moveaxis((codes * scale).reshape(v.shape), -1, axis)


WIDE = False


def mx_kscale(k):
    if not WIDE:
        return np.ones(k)
    levels = np.array([10, -10, 5, -5, 0])
    if k % 512:
        return np.exp2(np.random.permutation(np.resize(levels, k // 32))).repeat(32)
    a = np.empty((k // 512, 16))
    for p in range(k // 512):
        a[p, :8] = np.random.permutation(np.resize(levels, 8))
        for g in range(8):
            far = levels[np.abs(levels - a[p, g]) >= 10]
            a[p, g + 8] = far[np.random.randint(len(far))]
    return np.exp2(a.ravel()).repeat(32)


def f64(x):
    return np.asarray(x).astype(np.float64)


def striped(idx):
    return np.tile(idx.reshape(-1, 16).T, (8, 1)).astype(np.uint16)


def unstriped(offs):
    return offs[:16].T.reshape(-1).astype(np.int64)


E2M1 = np.array([0.0, 0.5, 1.0, 1.5, 2.0, 3.0, 4.0, 6.0, -0.0, -0.5, -1.0, -1.5, -2.0, -3.0, -4.0, -6.0])


def pack_weight(w, fmt):
    k, n = w.shape
    w = f64(np.asarray(w, np.float32).astype(ml_dtypes.bfloat16)).reshape(k // 32, 32, n)
    amax = np.abs(w).max(1)
    if fmt == "e4m3":
        byte = np.frexp(amax)[1] - 1 + 127 - 7
    else:
        mant, ex = np.frexp(amax / 6.0)
        byte = np.where(mant > 0.5, ex, ex - 1) + 127
    byte = np.clip(np.where(amax > 0, byte, 1), 1, 254)
    scaled = (w * np.exp2(127.0 - byte)[:, None, :]).reshape(k, n).astype(np.float32)
    by_word = np.ascontiguousarray(scaled.reshape(k // 512, 128, 4, n).transpose(0, 1, 3, 2))
    if fmt == "e4m3":
        words = by_word.astype(ml_dtypes.float8_e4m3fn).view(np.uint8)
    else:
        c = by_word.astype(ml_dtypes.float4_e2m1fn).view(np.uint8) & 0xF
        words = (c[..., 0::2] | (c[..., 1::2] << 4)).reshape(k // 512, 128, 2 * n)
    return np.ascontiguousarray(words), np.ascontiguousarray(byte.astype(np.uint8).reshape(k // 512, 16, n))


def unpack_weight(words, scales, fmt):
    g, _, n = scales.shape
    words = np.ascontiguousarray(words).reshape(g, 128, n, -1)
    if fmt == "e4m3":
        vals = words.view(ml_dtypes.float8_e4m3fn).astype(np.float64)
    else:
        nib = np.empty((g, 128, n, 4), np.uint8)
        nib[..., 0::2] = words & 0xF
        nib[..., 1::2] = words >> 4
        vals = E2M1[nib]
    vals = vals * np.repeat(np.exp2(scales.astype(np.float64) - 127.0), 8, axis=1)[..., None]
    return vals.transpose(0, 1, 3, 2).reshape(g * 512, n)


def gelu(v):
    return 0.5 * v * (1.0 + np.tanh(np.sqrt(2.0 / np.pi) * (v + 0.044715 * v**3)))


def twice(P):
    return np.random.permutation(np.repeat(np.arange(P), 2))


K, H, T, S, P = 512, 1536, 4096, 1024, 512


def setup_inputs():
    n = np.random.standard_normal
    s = mx_kscale(K)[:, None]
    u = mx_kscale(H)[:, None]
    d = {}
    d["tab_words"], d["tab_scales"] = pack_weight(n((K, T)) * s, "e4m3")
    d["offs"] = striped(np.random.permutation(T)[:S])
    d["pos1"] = striped(np.random.permutation(S)[:P])
    d["pos2"] = striped(np.random.permutation(S)[:P])
    d["pos3"] = striped(twice(P))
    d["w1"] = (n((K, H)) / K ** 0.5 / s * u.T).astype(np.float32)
    d["w2_words"], d["w2_scales"] = pack_weight(0.9 * n((H, H)) / H ** 0.5 / u, "e2m1")
    d["gain"] = (np.exp(0.3 * n(H)) / u[:, 0]).astype(np.float32)
    d["low"] = n(H).astype(np.float32)
    return d


def reference(tab_words, tab_scales, offs, pos1, pos2, pos3, w1, w2_words, w2_scales, gain, low):
    v = unpack_weight(tab_words, tab_scales, "e4m3")[:, unstriped(offs)]
    h = mxq(f64(w1), 0, "e4m3").T @ v
    x = np.abs(h[:, unstriped(pos1)]) + np.abs(h[:, unstriped(pos2)])
    w2 = unpack_weight(w2_words, w2_scales, "e2m1")
    y = w2.T @ mxq(x, 0, "e4m3")
    z = y[:, unstriped(pos3)] + f64(gain)[:, None] * h
    return np.maximum(z, f64(low)[:, None])

@@ -1,0 +1,272 @@
+from contextlib import ExitStack
+
+import concourse.mybir as mybir
+from concourse.masks import make_identity
+
+K, H, T, S, M = 512, 1536, 4096, 1024, 512
+FLOPS = 2 * K * H * S + 2 * H * H * M
+
+F32 = mybir.dt.float32
+BF16 = mybir.dt.bfloat16
+I32 = mybir.dt.int32
+U32 = mybir.dt.uint32
+U16 = mybir.dt.uint16
+U8 = mybir.dt.uint8
+FP8X4 = mybir.dt.float8_e4m3fn_x4
+FP4X4 = mybir.dt.float4_e2m1fn_x4
+ACT = mybir.ActivationFunctionType
+ALU = mybir.AluOpType
+
+P = 128
+PACK = 4
+BANK = 512
+TILES = H // P
+PASSES = H // (P * PACK)
+SPARE = 32
+W1_CHUNKS = (128, 128, 256, 512, 512)
+W1_ON_SCALAR = 2
+
+
+def tile_list_pearl_strand_lustre_kernel(tc, tab_words, tab_scales, offs, pos1, pos2, pos3, w1, w2_words, w2_scales, gain, low, out):
+    nc = tc.nc
+    with ExitStack() as ctx:
+        keep = ctx.enter_context(tc.tile_pool(name="keep", bufs=1))
+        ring = ctx.enter_context(tc.tile_pool(name="ring", bufs=2))
+        psum = ctx.enter_context(tc.psum_pool(name="psum", bufs=1))
+
+        offs_sb = keep.tile([P, S // 16], U16, name="offs_sb")
+        pos1_sb = keep.tile([P, M // 16], U16, name="pos1_sb")
+        pos2_sb = keep.tile([P, M // 16], U16, name="pos2_sb")
+        pos3_sb = keep.tile([P, S // 16], U16, name="pos3_sb")
+        table_words = keep.tile([P, T], I32, name="table_words", align_bytes=64)
+        table_scales = keep.tile([P, T], U8, name="table_scales", align_bytes=64)
+        w2_scale_sb = keep.tile([P, PASSES, H], U8, name="w2_scale_sb", align_bytes=64)
+        identity = keep.tile([P, P], F32, name="identity")
+        vector_rows = keep.tile([P, P], F32, name="vector_rows")
+
+        nc.vector.memset(table_scales[:].bitcast(I32), 0)
+        nc.vector.memset(w2_scale_sb[:].rearrange("p a n -> p (a n)").bitcast(I32), 0)
+        make_identity(nc, identity[:])
+        nc.gpsimd.memset(vector_rows[:], 0.0)
+        y_tiles = [keep.tile([P, M + SPARE], F32, name=f"y_tile{i}") for i in range(3)]
+        for y_tile in y_tiles:
+            nc.gpsimd.memset(y_tile[:, M:], 0.0)
+
+        starts = [sum(W1_CHUNKS[:i]) for i in range(len(W1_CHUNKS))]
+        w1_raw = [keep.tile([P, PACK, w], F32, name=f"w1_raw{i}") for i, w in enumerate(W1_CHUNKS)]
+        w1_view = w1.rearrange("(p j) n -> p j n", j=PACK)
+
+        def load_w1(i):
+            nc.sync.dma_start(out=w1_raw[i][:], in_=w1_view[:, :, starts[i] : starts[i] + W1_CHUNKS[i]])
+
+        nc.sync.dma_start(offs_sb[:], offs)
+        load_w1(0)
+        words_view = tab_words[0].rearrange("p t i -> p (t i)").bitcast(I32)
+        for half in range(2):
+            cols = slice(half * T // 2, (half + 1) * T // 2)
+            nc.sync.dma_start(out=table_words[:, cols], in_=words_view[:, cols])
+        for q in range(4):
+            nc.scalar.dma_start(
+                out=table_scales[32 * q : 32 * q + 4, :].bitcast(I32),
+                in_=tab_scales[0, 4 * q : 4 * q + 4, :].bitcast(I32),
+            )
+        load_w1(1)
+        nc.sync.dma_start(pos1_sb[:], pos1)
+        nc.sync.dma_start(pos2_sb[:], pos2)
+        for i in range(2, len(W1_CHUNKS)):
+            load_w1(i)
+        w2_sb = [keep.tile([P, 2 * H], U8, name=f"w2_sb{a}", align_bytes=64) for a in range(PASSES)]
+        for a in range(PASSES):
+            nc.sync.dma_start(out=w2_sb[a][:].bitcast(I32), in_=w2_words[a].bitcast(I32))
+        for q in range(4):
+            nc.sync.dma_start(
+                out=w2_scale_sb[32 * q : 32 * q + 4, :, :].bitcast(I32),
+                in_=w2_scales[:, 4 * q : 4 * q + 4, :].rearrange("a r n -> r a n").bitcast(I32),
+            )
+        nc.sync.dma_start(pos3_sb[:], pos3)
+        nc.sync.dma_start(out=vector_rows[0:TILES, :], in_=gain.rearrange("(c i) -> c i", i=P))
+        nc.sync.dma_start(out=vector_rows[TILES : 2 * TILES, :], in_=low.rearrange("(c i) -> c i", i=P))
+
+        w1_codes = [keep.tile([P, w], U32, name=f"w1_codes{i}", align_bytes=64) for i, w in enumerate(W1_CHUNKS)]
+        w1_scales = [keep.tile([P, w], U8, name=f"w1_scales{i}", align_bytes=64) for i, w in enumerate(W1_CHUNKS)]
+        w1_bf = [keep.tile([P, w, PACK], BF16, name=f"w1_bf{i}", align_bytes=64) for i, w in enumerate(W1_CHUNKS)]
+
+        def round_w1(i):
+            dst = w1_bf[i][:].rearrange("p (c e) j -> p c j e", e=4)
+            src = w1_raw[i][:].rearrange("p j (c e) -> p c j e", e=4)
+            if i < W1_ON_SCALAR:
+                nc.scalar.copy(out=dst, in_=src)
+            else:
+                nc.vector.tensor_copy(out=dst, in_=src)
+
+        def quantize_w1(i):
+            nc.vector.quantize_mx(
+                out=w1_codes[i][:].bitcast(FP8X4), scales=w1_scales[i][:], in_=w1_bf[i][:].rearrange("p n j -> p (n j)")
+            )
+
+        v_scales = keep.tile([P, S], U8, name="v_scales", align_bytes=64)
+        v_words = [keep.tile([P, BANK], I32, name=f"v_words{i}", align_bytes=64) for i in range(2)]
+        round_w1(0)
+        quantize_w1(0)
+        nc.vector.tensor_copy(v_scales[:], table_scales[:].indirect(offs_sb[:]))
+        for half in range(2):
+            nc.vector.tensor_copy(
+                v_words[half][:].bitcast(U32),
+                table_words[:].bitcast(U32).indirect(offs_sb[:, 32 * half : 32 * half + 32]),
+            )
+        round_w1(1)
+        quantize_w1(1)
+
+        h_tiles = [keep.tile([P, S], F32, name=f"h_tile{c}") for c in range(TILES)]
+
+        def make_h(c):
+            i = max(n for n in range(len(W1_CHUNKS)) if starts[n] <= P * c)
+            cols = slice(P * c - starts[i], P * (c + 1) - starts[i])
+            for half in range(2):
+                acc = psum.tile([P, BANK], F32, name="acc", tag="acc", bufs=3)
+                nc.tensor.matmul_mx(
+                    out=acc[:],
+                    lhsT=w1_codes[i][:, cols].bitcast(FP8X4),
+                    lhsT_scale=w1_scales[i][:, cols],
+                    rhs=v_words[half][:].bitcast(FP8X4),
+                    rhs_scale=v_scales[:, BANK * half : BANK * (half + 1)],
+                    start=True,
+                    stop=True,
+                )
+                nc.scalar.copy(out=h_tiles[c][:, BANK * half : BANK * (half + 1)], in_=acc[:])
+
+        picked = {}
+
+        def pick_h(c):
+            pair = [ring.tile([P, M], F32, name="picked", tag="picked", bufs=4) for which in range(2)]
+            pieces = 2 if c == TILES - 1 else 1
+            width = M // pieces
+            for piece in range(pieces):
+                for g, pos_sb in zip(pair, (pos1_sb, pos2_sb)):
+                    nc.vector.tensor_copy(
+                        g[:, width * piece : width * (piece + 1)],
+                        h_tiles[c][:].indirect(pos_sb[:, width // 16 * piece : width // 16 * (piece + 1)]),
+                    )
+            picked[c] = pair
+
+        mags = {}
+
+        def turn_and_abs(c, half):
+            a, q = divmod(c, 4)
+            if q == 0:
+                mags[a, half] = ring.tile([P, 4, PACK, P], F32, name="mags", tag=f"mags{half}", bufs=2)
+            turned = psum.tile([P, BANK], F32, name="turned", tag="turned", bufs=3)
+            for s in range(4):
+                b, which = 2 * half + s // 2, s % 2
+                nc.tensor.transpose(turned[:, P * s : P * (s + 1)], picked[c][which][:, P * b : P * (b + 1)], identity[:])
+            nc.scalar.activation(
+                out=mags[a, half][:, :, :, 32 * q : 32 * q + 32],
+                in_=turned[:].rearrange("m (s p t) -> m s t p", s=4, t=PACK),
+                func=ACT.Abs,
+            )
+
+        x_bf = {}
+        x_codes = [keep.tile([P, M], U32, name=f"x_codes{a}", align_bytes=64) for a in range(PASSES)]
+        x_scales = [keep.tile([P, M], U8, name=f"x_scales{a}", align_bytes=64) for a in range(PASSES)]
+
+        def sum_x(a, b):
+            half, inner = divmod(b, 2)
+            if inner == 0:
+                x_bf[a, half] = ring.tile([P, M // 2, PACK], BF16, name="x_bf", tag="x_bf", bufs=3, align_bytes=64)
+            summed = psum.tile([P, PACK, P], F32, name="summed", tag="summed", bufs=2)
+            for t in range(PACK):
+                for which in range(2):
+                    nc.tensor.matmul(
+                        summed[:, t, :],
+                        mags[a, half][:, 2 * inner + which, t, :],
+                        identity[:],
+                        start=(which == 0),
+                        stop=(which == 1),
+                        is_transpose=True,
+                    )
+            dst = x_bf[a, half][:, P * inner : P * (inner + 1), :]
+            src = summed[:].rearrange("p t m -> p m t")
+            if a == PASSES - 1 and inner == 1:
+                nc.vector.tensor_copy(out=dst, in_=src)
+            else:
+                nc.scalar.copy(out=dst, in_=src)
+
+        def quantize_x(a, half):
+            cols = slice(half * M // 2, (half + 1) * M // 2)
+            nc.vector.quantize_mx(
+                out=x_codes[a][:, cols].bitcast(FP8X4), scales=x_scales[a][:, cols], in_=x_bf[a, half][:].rearrange("p m t -> p (m t)")
+            )
+
+        make_h(0)
+        for c in range(TILES + 1):
+            if c + 1 < TILES:
+                make_h(c + 1)
+            if c < TILES:
+                pick_h(c)
+            if c + 2 < len(W1_CHUNKS):
+                round_w1(c + 2)
+            if c >= 5:
+                sum_x(*divmod(c - 5, 4))
+            if c >= 1:
+                turn_and_abs(c - 1, 0)
+                turn_and_abs(c - 1, 1)
+            if c + 2 < len(W1_CHUNKS):
+                quantize_w1(c + 2)
+            if c >= 7 and c % 2 == 1:
+                quantize_x(*divmod((c - 7) // 2, 2))
+        quantize_x(1, 1)
+        for half in range(2):
+            sum_x(PASSES - 1, 2 * half)
+            sum_x(PASSES - 1, 2 * half + 1)
+            quantize_x(PASSES - 1, half)
+
+        columns = keep.tile([P, 2 * TILES], F32, name="columns")
+        turned = psum.tile([P, BANK], F32, name="turned", tag="turned", bufs=3)
+        nc.tensor.transpose(turned[:, 0:P], vector_rows[:], identity[:])
+        nc.scalar.copy(out=columns[:], in_=turned[:, 0 : 2 * TILES])
+
+        scaled = {}
+
+        def make_y(c):
+            acc = psum.tile([P, BANK], F32, name="acc", tag="acc", bufs=3)
+            for a in range(PASSES):
+                nc.tensor.matmul_mx(
+                    out=acc[:],
+                    lhsT=w2_sb[a][:, 2 * P * c : 2 * P * (c + 1)].bitcast(FP4X4),
+                    lhsT_scale=w2_scale_sb[:, a, P * c : P * (c + 1)],
+                    rhs=x_codes[a][:].bitcast(FP8X4),
+                    rhs_scale=x_scales[a][:],
+                    start=(a == 0),
+                    stop=(a == PASSES - 1),
+                )
+            nc.scalar.copy(out=y_tiles[c % 3][:, 0:M], in_=acc[:])
+            scaled[c] = ring.tile([P, S], F32, name="scaled", tag="scaled", bufs=3)
+            nc.scalar.activation(out=scaled[c][:], in_=h_tiles[c][:], func=ACT.Copy, scale=columns[:, c : c + 1])
+
+        sums = {}
+
+        def add_y(c, half):
+            z = ring.tile([P, BANK], F32, name="z", tag="z", bufs=3)
+            nc.vector.tensor_tensor(
+                z[:],
+                y_tiles[c % 3][:].indirect(pos3_sb[:, 32 * half : 32 * half + 32]),
+                scaled[c][:, BANK * half : BANK * (half + 1)],
+                ALU.add,
+            )
+            sums[c, half] = z
+
+        def finish(c, half):
+            res = ring.tile([P, BANK], F32, name="res", tag="res", bufs=4)
+            nc.vector.tensor_scalar_max(res[:], sums[c, half][:], columns[:, TILES + c : TILES + c + 1])
+            nc.sync.dma_start(out=out[P * c : P * (c + 1), BANK * half : BANK * (half + 1)], in_=res[:])
+
+        make_y(0)
+        make_y(1)
+        for step in range(2 * TILES + 1):
+            c, half = divmod(step, 2)
+            if c < TILES:
+                add_y(c, half)
+            if step >= 1:
+                finish(*divmod(step - 1, 2))
+            if half == 1 and c + 2 < TILES:
+                make_y(c + 2)

@@ -24,7 +24,7 @@ TILES = H // P
 PASSES = H // (P * PACK)
 SPARE = 32
 W1_CHUNKS = (128, 128, 256, 512, 512)
-W1_ON_SCALAR = 2
+W1_ON_SCALAR = 3
 
 
 def tile_list_pearl_strand_lustre_kernel(tc, tab_words, tab_scales, offs, pos1, pos2, pos3, w1, w2_words, w2_scales, gain, low, out):
@@ -114,8 +114,9 @@ def tile_list_pearl_strand_lustre_kernel(tc, tab_words, tab_scales, offs, pos1, 
                 v_words[half][:].bitcast(U32),
                 table_words[:].bitcast(U32).indirect(offs_sb[:, 32 * half : 32 * half + 32]),
             )
-        round_w1(1)
-        quantize_w1(1)
+        for i in (1, 2):
+            round_w1(i)
+            quantize_w1(i)
 
         h_tiles = [keep.tile([P, S], F32, name=f"h_tile{c}") for c in range(TILES)]
 
@@ -135,93 +136,98 @@ def tile_list_pearl_strand_lustre_kernel(tc, tab_words, tab_scales, offs, pos1, 
                 )
                 nc.scalar.copy(out=h_tiles[c][:, BANK * half : BANK * (half + 1)], in_=acc[:])
 
-        picked = {}
-
-        def pick_h(c):
-            pair = [ring.tile([P, M], F32, name="picked", tag="picked", bufs=4) for which in range(2)]
-            pieces = 2 if c == TILES - 1 else 1
-            width = M // pieces
-            for piece in range(pieces):
-                for g, pos_sb in zip(pair, (pos1_sb, pos2_sb)):
-                    nc.vector.tensor_copy(
-                        g[:, width * piece : width * (piece + 1)],
-                        h_tiles[c][:].indirect(pos_sb[:, width // 16 * piece : width // 16 * (piece + 1)]),
-                    )
-            picked[c] = pair
-
+        whole, tapered = ((0, 4),), ((0, 2), (2, 3), (3, 4))
         mags = {}
 
-        def turn_and_abs(c, half):
+        def pick_h(c):
+            picked = ring.tile([P, 2, M], F32, name="picked", tag="picked", bufs=3)
+            mags[c] = ring.tile([P, 2, M], F32, name="mags", tag="mags", bufs=3)
+            for b0, b1 in tapered if c == TILES - 1 else whole:
+                cols = slice(P * b0, P * b1)
+                for which, pos_sb in enumerate((pos1_sb, pos2_sb)):
+                    nc.vector.tensor_copy(picked[:, which, cols], h_tiles[c][:].indirect(pos_sb[:, 8 * b0 : 8 * b1]))
+                nc.scalar.activation(out=mags[c][:, :, cols], in_=picked[:, :, cols], func=ACT.Abs)
+
+        x_rows = {}
+
+        def sum_x(c):
             a, q = divmod(c, 4)
-            if q == 0:
-                mags[a, half] = ring.tile([P, 4, PACK, P], F32, name="mags", tag=f"mags{half}", bufs=2)
-            turned = psum.tile([P, BANK], F32, name="turned", tag="turned", bufs=3)
-            for s in range(4):
-                b, which = 2 * half + s // 2, s % 2
-                nc.tensor.transpose(turned[:, P * s : P * (s + 1)], picked[c][which][:, P * b : P * (b + 1)], identity[:])
-            nc.scalar.activation(
-                out=mags[a, half][:, :, :, 32 * q : 32 * q + 32],
-                in_=turned[:].rearrange("m (s p t) -> m s t p", s=4, t=PACK),
-                func=ACT.Abs,
-            )
+            for b0, b1 in tapered if a == PASSES - 1 else whole:
+                if q == 0:
+                    x_rows[a, b0] = ring.tile([P, b1 - b0, 2, P, 2], BF16, name="x_rows", tag=f"x_rows{b1 - b0}", bufs=2)
+                summed = psum.tile([P, b1 - b0, P], F32, name="summed", tag="summed", bufs=3)
+                for b in range(b0, b1):
+                    for which in range(2):
+                        nc.tensor.matmul(
+                            summed[:, b - b0, :],
+                            mags[c][:, which, P * b : P * (b + 1)],
+                            identity[:],
+                            start=(which == 0),
+                            stop=(which == 1),
+                            is_transpose=True,
+                        )
+                nc.scalar.copy(
+                    out=x_rows[a, b0][:, :, :, 32 * q : 32 * q + 32, :],
+                    in_=summed[:].rearrange("m b (p u e) -> m b u p e", u=2, e=2),
+                )
 
         x_bf = {}
         x_codes = [keep.tile([P, M], U32, name=f"x_codes{a}", align_bytes=64) for a in range(PASSES)]
         x_scales = [keep.tile([P, M], U8, name=f"x_scales{a}", align_bytes=64) for a in range(PASSES)]
 
-        def sum_x(a, b):
-            half, inner = divmod(b, 2)
-            if inner == 0:
-                x_bf[a, half] = ring.tile([P, M // 2, PACK], BF16, name="x_bf", tag="x_bf", bufs=3, align_bytes=64)
-            summed = psum.tile([P, PACK, P], F32, name="summed", tag="summed", bufs=2)
-            for t in range(PACK):
-                for which in range(2):
-                    nc.tensor.matmul(
-                        summed[:, t, :],
-                        mags[a, half][:, 2 * inner + which, t, :],
-                        identity[:],
-                        start=(which == 0),
-                        stop=(which == 1),
-                        is_transpose=True,
-                    )
-            dst = x_bf[a, half][:, P * inner : P * (inner + 1), :]
-            src = summed[:].rearrange("p t m -> p m t")
-            if a == PASSES - 1 and inner == 1:
+        turned_x = {}
+
+        def turn_x(a, b0, b1):
+            first = b0 if a == PASSES - 1 else 0
+            words = x_rows[a, first][:].rearrange("m b u p e -> m b u (p e)").bitcast(F32)
+            turned = psum.tile([P, b1 - b0, 2, P], F32, name="turned", tag="turned", bufs=2)
+            for b in range(b0, b1):
+                for u in range(2):
+                    nc.tensor.transpose(turned[:, b - b0, u, :], words[:, b - first, u, :], identity[:])
+            turned_x[a, b0] = turned
+
+        def weave_x(a, b0, b1, on_vector):
+            turned = turned_x[a, b0]
+            x_bf[a, b0] = ring.tile([P, (b1 - b0) * P * PACK], BF16, name="x_bf", tag="x_bf", bufs=3, align_bytes=64)
+            dst = x_bf[a, b0][:].bitcast(F32).rearrange("p (b m u) -> p b m u", m=P, u=2)
+            src = turned[:].rearrange("p b u m -> p b m u")
+            if on_vector:
                 nc.vector.tensor_copy(out=dst, in_=src)
             else:
                 nc.scalar.copy(out=dst, in_=src)
 
-        def quantize_x(a, half):
-            cols = slice(half * M // 2, (half + 1) * M // 2)
-            nc.vector.quantize_mx(
-                out=x_codes[a][:, cols].bitcast(FP8X4), scales=x_scales[a][:, cols], in_=x_bf[a, half][:].rearrange("p m t -> p (m t)")
-            )
+        def quantize_x(a, b0, b1):
+            cols = slice(P * b0, P * b1)
+            nc.vector.quantize_mx(out=x_codes[a][:, cols].bitcast(FP8X4), scales=x_scales[a][:, cols], in_=x_bf[a, b0][:])
 
         make_h(0)
-        for c in range(TILES + 1):
+        for c in range(TILES):
+            turning = c >= 5 and (c - 5) % 4 < 2
             if c + 1 < TILES:
                 make_h(c + 1)
-            if c < TILES:
-                pick_h(c)
-            if c + 2 < len(W1_CHUNKS):
-                round_w1(c + 2)
-            if c >= 5:
-                sum_x(*divmod(c - 5, 4))
+            if turning:
+                a, half = divmod(c - 5, 4)
+                turn_x(a, 2 * half, 2 * half + 2)
             if c >= 1:
-                turn_and_abs(c - 1, 0)
-                turn_and_abs(c - 1, 1)
-            if c + 2 < len(W1_CHUNKS):
-                quantize_w1(c + 2)
-            if c >= 7 and c % 2 == 1:
-                quantize_x(*divmod((c - 7) // 2, 2))
-        quantize_x(1, 1)
-        for half in range(2):
-            sum_x(PASSES - 1, 2 * half)
-            sum_x(PASSES - 1, 2 * half + 1)
-            quantize_x(PASSES - 1, half)
+                sum_x(c - 1)
+            pick_h(c)
+            if turning:
+                weave_x(a, 2 * half, 2 * half + 2, half == 1)
+            if c in (1, 4):
+                round_w1(3 + c // 4)
+            if c >= 6 and (c - 6) % 4 < 2:
+                a, half = divmod(c - 6, 4)
+                quantize_x(a, 2 * half, 2 * half + 2)
+            if c in (2, 5):
+                quantize_w1(3 + c // 4)
+        sum_x(TILES - 1)
+        for b0, b1 in tapered:
+            turn_x(PASSES - 1, b0, b1)
+            weave_x(PASSES - 1, b0, b1, True)
+            quantize_x(PASSES - 1, b0, b1)
 
         columns = keep.tile([P, 2 * TILES], F32, name="columns")
-        turned = psum.tile([P, BANK], F32, name="turned", tag="turned", bufs=3)
+        turned = psum.tile([P, BANK], F32, name="turned", tag="turned", bufs=2)
         nc.tensor.transpose(turned[:, 0:P], vector_rows[:], identity[:])
         nc.scalar.copy(out=columns[:], in_=turned[:, 0 : 2 * TILES])
 

@@ -20,11 +20,20 @@ ALU = mybir.AluOpType
 P = 128
 PACK = 4
 BANK = 512
+GROUP = 16
+QUADRANT = 32
 TILES = H // P
 PASSES = H // (P * PACK)
-SPARE = 32
+Y_WINDOW = S + 32
+Y_TILES = 3
 W1_CHUNKS = (128, 128, 256, 512, 512)
 W1_ON_SCALAR = 3
+W1_ROUND_STEP = {1: 3, 4: 4}
+SCALED_ON_VECTOR = 3
+
+ALL_BLOCKS = ((0, 4),)
+BLOCK_PAIRS = ((0, 2), (2, 4))
+SHRINKING_BLOCKS = ((0, 2), (2, 3), (3, 4))
 
 
 def tile_list_pearl_strand_lustre_kernel(tc, tab_words, tab_scales, offs, pos1, pos2, pos3, w1, w2_words, w2_scales, gain, low, out):
@@ -34,41 +43,41 @@ def tile_list_pearl_strand_lustre_kernel(tc, tab_words, tab_scales, offs, pos1, 
         ring = ctx.enter_context(tc.tile_pool(name="ring", bufs=2))
         psum = ctx.enter_context(tc.psum_pool(name="psum", bufs=1))
 
-        offs_sb = keep.tile([P, S // 16], U16, name="offs_sb")
-        pos1_sb = keep.tile([P, M // 16], U16, name="pos1_sb")
-        pos2_sb = keep.tile([P, M // 16], U16, name="pos2_sb")
-        pos3_sb = keep.tile([P, S // 16], U16, name="pos3_sb")
+        offs_sb = keep.tile([P, S // GROUP], U16, name="offs_sb")
+        pos1_sb = keep.tile([P, M // GROUP], U16, name="pos1_sb")
+        pos2_sb = keep.tile([P, M // GROUP], U16, name="pos2_sb")
+        pos3_sb = keep.tile([P, S // GROUP], U16, name="pos3_sb")
         table_words = keep.tile([P, T], I32, name="table_words", align_bytes=64)
         table_scales = keep.tile([P, T], U8, name="table_scales", align_bytes=64)
         w2_scale_sb = keep.tile([P, PASSES, H], U8, name="w2_scale_sb", align_bytes=64)
         identity = keep.tile([P, P], F32, name="identity")
         vector_rows = keep.tile([P, P], F32, name="vector_rows")
+        y_tiles = [keep.tile([P, Y_WINDOW], F32, name=f"y_tile{i}") for i in range(Y_TILES)]
 
         nc.vector.memset(table_scales[:].bitcast(I32), 0)
         nc.vector.memset(w2_scale_sb[:].rearrange("p a n -> p (a n)").bitcast(I32), 0)
-        make_identity(nc, identity[:])
-        nc.gpsimd.memset(vector_rows[:], 0.0)
-        y_tiles = [keep.tile([P, M + SPARE], F32, name=f"y_tile{i}") for i in range(3)]
+        nc.vector.memset(vector_rows[:], 0.0)
         for y_tile in y_tiles:
-            nc.gpsimd.memset(y_tile[:, M:], 0.0)
+            nc.vector.memset(y_tile[:, M:], 0.0)
+        make_identity(nc, identity[:])
 
-        starts = [sum(W1_CHUNKS[:i]) for i in range(len(W1_CHUNKS))]
-        w1_raw = [keep.tile([P, PACK, w], F32, name=f"w1_raw{i}") for i, w in enumerate(W1_CHUNKS)]
-        w1_view = w1.rearrange("(p j) n -> p j n", j=PACK)
+        w1_starts = [sum(W1_CHUNKS[:i]) for i in range(len(W1_CHUNKS))]
+        w1_raw = [keep.tile([P, PACK, width], F32, name=f"w1_raw{i}") for i, width in enumerate(W1_CHUNKS)]
+        w1_by_partition = w1.rearrange("(p t) r -> p t r", t=PACK)
 
         def load_w1(i):
-            nc.sync.dma_start(out=w1_raw[i][:], in_=w1_view[:, :, starts[i] : starts[i] + W1_CHUNKS[i]])
+            nc.sync.dma_start(out=w1_raw[i][:], in_=w1_by_partition[:, :, w1_starts[i] : w1_starts[i] + W1_CHUNKS[i]])
 
         nc.sync.dma_start(offs_sb[:], offs)
         load_w1(0)
-        words_view = tab_words[0].rearrange("p t i -> p (t i)").bitcast(I32)
-        for half in range(2):
-            cols = slice(half * T // 2, (half + 1) * T // 2)
-            nc.sync.dma_start(out=table_words[:, cols], in_=words_view[:, cols])
-        for q in range(4):
+        table_in_hbm = tab_words[0].rearrange("p t i -> p (t i)").bitcast(I32)
+        for first_column in (0, T // 2):
+            cols = slice(first_column, first_column + T // 2)
+            nc.sync.dma_start(out=table_words[:, cols], in_=table_in_hbm[:, cols])
+        for q in range(P // QUADRANT):
             nc.scalar.dma_start(
-                out=table_scales[32 * q : 32 * q + 4, :].bitcast(I32),
-                in_=tab_scales[0, 4 * q : 4 * q + 4, :].bitcast(I32),
+                out=table_scales[QUADRANT * q : QUADRANT * q + PACK, :].bitcast(I32),
+                in_=tab_scales[0, PACK * q : PACK * (q + 1), :].bitcast(I32),
             )
         load_w1(1)
         nc.sync.dma_start(pos1_sb[:], pos1)
@@ -78,22 +87,22 @@ def tile_list_pearl_strand_lustre_kernel(tc, tab_words, tab_scales, offs, pos1, 
         w2_sb = [keep.tile([P, 2 * H], U8, name=f"w2_sb{a}", align_bytes=64) for a in range(PASSES)]
         for a in range(PASSES):
             nc.sync.dma_start(out=w2_sb[a][:].bitcast(I32), in_=w2_words[a].bitcast(I32))
-        for q in range(4):
+        for q in range(P // QUADRANT):
             nc.sync.dma_start(
-                out=w2_scale_sb[32 * q : 32 * q + 4, :, :].bitcast(I32),
-                in_=w2_scales[:, 4 * q : 4 * q + 4, :].rearrange("a r n -> r a n").bitcast(I32),
+                out=w2_scale_sb[QUADRANT * q : QUADRANT * q + PACK, :, :].bitcast(I32),
+                in_=w2_scales[:, PACK * q : PACK * (q + 1), :].rearrange("a s n -> s a n").bitcast(I32),
             )
         nc.sync.dma_start(pos3_sb[:], pos3)
         nc.sync.dma_start(out=vector_rows[0:TILES, :], in_=gain.rearrange("(c i) -> c i", i=P))
         nc.sync.dma_start(out=vector_rows[TILES : 2 * TILES, :], in_=low.rearrange("(c i) -> c i", i=P))
 
-        w1_codes = [keep.tile([P, w], U32, name=f"w1_codes{i}", align_bytes=64) for i, w in enumerate(W1_CHUNKS)]
-        w1_scales = [keep.tile([P, w], U8, name=f"w1_scales{i}", align_bytes=64) for i, w in enumerate(W1_CHUNKS)]
-        w1_bf = [keep.tile([P, w, PACK], BF16, name=f"w1_bf{i}", align_bytes=64) for i, w in enumerate(W1_CHUNKS)]
+        w1_codes = [keep.tile([P, width], U32, name=f"w1_codes{i}", align_bytes=64) for i, width in enumerate(W1_CHUNKS)]
+        w1_scales = [keep.tile([P, width], U8, name=f"w1_scales{i}", align_bytes=64) for i, width in enumerate(W1_CHUNKS)]
+        w1_bf = [keep.tile([P, width, PACK], BF16, name=f"w1_bf{i}", align_bytes=64) for i, width in enumerate(W1_CHUNKS)]
 
         def round_w1(i):
-            dst = w1_bf[i][:].rearrange("p (c e) j -> p c j e", e=4)
-            src = w1_raw[i][:].rearrange("p j (c e) -> p c j e", e=4)
+            dst = w1_bf[i][:].rearrange("p (r e) t -> p r t e", e=4)
+            src = w1_raw[i][:].rearrange("p t (r e) -> p r t e", e=4)
             if i < W1_ON_SCALAR:
                 nc.scalar.copy(out=dst, in_=src)
             else:
@@ -101,58 +110,58 @@ def tile_list_pearl_strand_lustre_kernel(tc, tab_words, tab_scales, offs, pos1, 
 
         def quantize_w1(i):
             nc.vector.quantize_mx(
-                out=w1_codes[i][:].bitcast(FP8X4), scales=w1_scales[i][:], in_=w1_bf[i][:].rearrange("p n j -> p (n j)")
+                out=w1_codes[i][:].bitcast(FP8X4), scales=w1_scales[i][:], in_=w1_bf[i][:].rearrange("p r t -> p (r t)")
             )
 
         v_scales = keep.tile([P, S], U8, name="v_scales", align_bytes=64)
-        v_words = [keep.tile([P, BANK], I32, name=f"v_words{i}", align_bytes=64) for i in range(2)]
+        v_words = [keep.tile([P, BANK], I32, name=f"v_words{i}", align_bytes=64) for i in range(S // BANK)]
         round_w1(0)
         quantize_w1(0)
         nc.vector.tensor_copy(v_scales[:], table_scales[:].indirect(offs_sb[:]))
-        for half in range(2):
+        for i, j0 in enumerate(range(0, S, BANK)):
             nc.vector.tensor_copy(
-                v_words[half][:].bitcast(U32),
-                table_words[:].bitcast(U32).indirect(offs_sb[:, 32 * half : 32 * half + 32]),
+                v_words[i][:].bitcast(U32),
+                table_words[:].bitcast(U32).indirect(offs_sb[:, j0 // GROUP : (j0 + BANK) // GROUP]),
             )
-        for i in (1, 2):
+        for i in range(1, W1_ON_SCALAR):
             round_w1(i)
             quantize_w1(i)
 
         h_tiles = [keep.tile([P, S], F32, name=f"h_tile{c}") for c in range(TILES)]
 
         def make_h(c):
-            i = max(n for n in range(len(W1_CHUNKS)) if starts[n] <= P * c)
-            cols = slice(P * c - starts[i], P * (c + 1) - starts[i])
-            for half in range(2):
+            chunk = max(i for i, start in enumerate(w1_starts) if start <= P * c)
+            cols = slice(P * c - w1_starts[chunk], P * (c + 1) - w1_starts[chunk])
+            for i, j0 in enumerate(range(0, S, BANK)):
                 acc = psum.tile([P, BANK], F32, name="acc", tag="acc", bufs=3)
                 nc.tensor.matmul_mx(
                     out=acc[:],
-                    lhsT=w1_codes[i][:, cols].bitcast(FP8X4),
-                    lhsT_scale=w1_scales[i][:, cols],
-                    rhs=v_words[half][:].bitcast(FP8X4),
-                    rhs_scale=v_scales[:, BANK * half : BANK * (half + 1)],
+                    lhsT=w1_codes[chunk][:, cols].bitcast(FP8X4),
+                    lhsT_scale=w1_scales[chunk][:, cols],
+                    rhs=v_words[i][:].bitcast(FP8X4),
+                    rhs_scale=v_scales[:, j0 : j0 + BANK],
                     start=True,
                     stop=True,
                 )
-                nc.scalar.copy(out=h_tiles[c][:, BANK * half : BANK * (half + 1)], in_=acc[:])
+                nc.scalar.copy(out=h_tiles[c][:, j0 : j0 + BANK], in_=acc[:])
 
-        whole, tapered = ((0, 4),), ((0, 2), (2, 3), (3, 4))
-        mags = {}
+        magnitudes = {}
 
         def pick_h(c):
             picked = ring.tile([P, 2, M], F32, name="picked", tag="picked", bufs=3)
-            mags[c] = ring.tile([P, 2, M], F32, name="mags", tag="mags", bufs=3)
-            for b0, b1 in tapered if c == TILES - 1 else whole:
+            magnitudes[c] = ring.tile([P, 2, M], F32, name="magnitudes", tag="magnitudes", bufs=3)
+            for b0, b1 in SHRINKING_BLOCKS if c == TILES - 1 else ALL_BLOCKS:
                 cols = slice(P * b0, P * b1)
                 for which, pos_sb in enumerate((pos1_sb, pos2_sb)):
-                    nc.vector.tensor_copy(picked[:, which, cols], h_tiles[c][:].indirect(pos_sb[:, 8 * b0 : 8 * b1]))
-                nc.scalar.activation(out=mags[c][:, :, cols], in_=picked[:, :, cols], func=ACT.Abs)
+                    offsets = pos_sb[:, P * b0 // GROUP : P * b1 // GROUP]
+                    nc.vector.tensor_copy(picked[:, which, cols], h_tiles[c][:].indirect(offsets))
+                nc.scalar.activation(out=magnitudes[c][:, :, cols], in_=picked[:, :, cols], func=ACT.Abs)
 
         x_rows = {}
 
         def sum_x(c):
-            a, q = divmod(c, 4)
-            for b0, b1 in tapered if a == PASSES - 1 else whole:
+            a, q = divmod(c, PACK)
+            for b0, b1 in BLOCK_PAIRS if a == PASSES - 1 else ALL_BLOCKS:
                 if q == 0:
                     x_rows[a, b0] = ring.tile([P, b1 - b0, 2, P, 2], BF16, name="x_rows", tag=f"x_rows{b1 - b0}", bufs=2)
                 summed = psum.tile([P, b1 - b0, P], F32, name="summed", tag="summed", bufs=3)
@@ -160,38 +169,34 @@ def tile_list_pearl_strand_lustre_kernel(tc, tab_words, tab_scales, offs, pos1, 
                     for which in range(2):
                         nc.tensor.matmul(
                             summed[:, b - b0, :],
-                            mags[c][:, which, P * b : P * (b + 1)],
+                            magnitudes[c][:, which, P * b : P * (b + 1)],
                             identity[:],
                             start=(which == 0),
                             stop=(which == 1),
                             is_transpose=True,
                         )
                 nc.scalar.copy(
-                    out=x_rows[a, b0][:, :, :, 32 * q : 32 * q + 32, :],
+                    out=x_rows[a, b0][:, :, :, QUADRANT * q : QUADRANT * (q + 1), :],
                     in_=summed[:].rearrange("m b (p u e) -> m b u p e", u=2, e=2),
                 )
 
-        x_bf = {}
+        x_turned, x_bf = {}, {}
         x_codes = [keep.tile([P, M], U32, name=f"x_codes{a}", align_bytes=64) for a in range(PASSES)]
         x_scales = [keep.tile([P, M], U8, name=f"x_scales{a}", align_bytes=64) for a in range(PASSES)]
 
-        turned_x = {}
-
         def turn_x(a, b0, b1):
-            first = b0 if a == PASSES - 1 else 0
-            words = x_rows[a, first][:].rearrange("m b u p e -> m b u (p e)").bitcast(F32)
-            turned = psum.tile([P, b1 - b0, 2, P], F32, name="turned", tag="turned", bufs=2)
+            first_block = b0 if a == PASSES - 1 else 0
+            words = x_rows[a, first_block][:].rearrange("m b u p e -> m b u (p e)").bitcast(F32)
+            x_turned[a, b0] = psum.tile([P, b1 - b0, 2, P], F32, name="turned", tag="turned", bufs=2)
             for b in range(b0, b1):
                 for u in range(2):
-                    nc.tensor.transpose(turned[:, b - b0, u, :], words[:, b - first, u, :], identity[:])
-            turned_x[a, b0] = turned
+                    nc.tensor.transpose(x_turned[a, b0][:, b - b0, u, :], words[:, b - first_block, u, :], identity[:])
 
-        def weave_x(a, b0, b1, on_vector):
-            turned = turned_x[a, b0]
-            x_bf[a, b0] = ring.tile([P, (b1 - b0) * P * PACK], BF16, name="x_bf", tag="x_bf", bufs=3, align_bytes=64)
+        def weave_x(a, b0, b1):
+            x_bf[a, b0] = ring.tile([P, (b1 - b0) * P * PACK], BF16, name="x_bf", tag="staged", bufs=2, align_bytes=64)
             dst = x_bf[a, b0][:].bitcast(F32).rearrange("p (b m u) -> p b m u", m=P, u=2)
-            src = turned[:].rearrange("p b u m -> p b m u")
-            if on_vector:
+            src = x_turned[a, b0][:].rearrange("p b u m -> p b m u")
+            if a == PASSES - 1 and b0 > 0:
                 nc.vector.tensor_copy(out=dst, in_=src)
             else:
                 nc.scalar.copy(out=dst, in_=src)
@@ -200,38 +205,40 @@ def tile_list_pearl_strand_lustre_kernel(tc, tab_words, tab_scales, offs, pos1, 
             cols = slice(P * b0, P * b1)
             nc.vector.quantize_mx(out=x_codes[a][:, cols].bitcast(FP8X4), scales=x_scales[a][:, cols], in_=x_bf[a, b0][:])
 
+        turn_at = {PACK * a + PACK + 1 + i: (a, *pair) for a in range(PASSES - 1) for i, pair in enumerate(BLOCK_PAIRS)}
         make_h(0)
         for c in range(TILES):
-            turning = c >= 5 and (c - 5) % 4 < 2
             if c + 1 < TILES:
                 make_h(c + 1)
-            if turning:
-                a, half = divmod(c - 5, 4)
-                turn_x(a, 2 * half, 2 * half + 2)
+            if c in turn_at:
+                turn_x(*turn_at[c])
             if c >= 1:
                 sum_x(c - 1)
             pick_h(c)
-            if turning:
-                weave_x(a, 2 * half, 2 * half + 2, half == 1)
-            if c in (1, 4):
-                round_w1(3 + c // 4)
-            if c >= 6 and (c - 6) % 4 < 2:
-                a, half = divmod(c - 6, 4)
-                quantize_x(a, 2 * half, 2 * half + 2)
-            if c in (2, 5):
-                quantize_w1(3 + c // 4)
+            if c in turn_at:
+                weave_x(*turn_at[c])
+            if c in W1_ROUND_STEP:
+                round_w1(W1_ROUND_STEP[c])
+            if c - 1 in turn_at:
+                quantize_x(*turn_at[c - 1])
+            if c - 1 in W1_ROUND_STEP:
+                quantize_w1(W1_ROUND_STEP[c - 1])
         sum_x(TILES - 1)
-        for b0, b1 in tapered:
-            turn_x(PASSES - 1, b0, b1)
-            weave_x(PASSES - 1, b0, b1, True)
-            quantize_x(PASSES - 1, b0, b1)
 
         columns = keep.tile([P, 2 * TILES], F32, name="columns")
-        turned = psum.tile([P, BANK], F32, name="turned", tag="turned", bufs=2)
-        nc.tensor.transpose(turned[:, 0:P], vector_rows[:], identity[:])
-        nc.scalar.copy(out=columns[:], in_=turned[:, 0 : 2 * TILES])
-
+        vector_columns = psum.tile([P, P], F32, name="vector_columns", tag="summed", bufs=3)
+        nc.tensor.transpose(vector_columns[:], vector_rows[:], identity[:])
+        nc.vector.tensor_copy(out=columns[:], in_=vector_columns[:, 0 : 2 * TILES])
         scaled = {}
+        for c in range(SCALED_ON_VECTOR):
+            nc.vector.tensor_scalar_mul(h_tiles[c][:], h_tiles[c][:], columns[:, c : c + 1])
+            scaled[c] = h_tiles[c]
+
+        for b0, b1 in BLOCK_PAIRS:
+            turn_x(PASSES - 1, b0, b1)
+            weave_x(PASSES - 1, b0, b1)
+        for b0, b1 in BLOCK_PAIRS:
+            quantize_x(PASSES - 1, b0, b1)
 
         def make_y(c):
             acc = psum.tile([P, BANK], F32, name="acc", tag="acc", bufs=3)
@@ -245,34 +252,32 @@ def tile_list_pearl_strand_lustre_kernel(tc, tab_words, tab_scales, offs, pos1, 
                     start=(a == 0),
                     stop=(a == PASSES - 1),
                 )
-            nc.scalar.copy(out=y_tiles[c % 3][:, 0:M], in_=acc[:])
-            scaled[c] = ring.tile([P, S], F32, name="scaled", tag="scaled", bufs=3)
+            nc.scalar.copy(out=y_tiles[c % Y_TILES][:, 0:M], in_=acc[:])
+
+        def scale_h(c):
+            scaled[c] = ring.tile([P, S], F32, name="scaled", tag="staged", bufs=2, align_bytes=64)
             nc.scalar.activation(out=scaled[c][:], in_=h_tiles[c][:], func=ACT.Copy, scale=columns[:, c : c + 1])
 
-        sums = {}
+        results = {}
 
-        def add_y(c, half):
-            z = ring.tile([P, BANK], F32, name="z", tag="z", bufs=3)
-            nc.vector.tensor_tensor(
-                z[:],
-                y_tiles[c % 3][:].indirect(pos3_sb[:, 32 * half : 32 * half + 32]),
-                scaled[c][:, BANK * half : BANK * (half + 1)],
-                ALU.add,
-            )
-            sums[c, half] = z
+        def add_y(c, j0, j1):
+            results[c, j0] = ring.tile([P, j1 - j0], F32, name="results", tag="results", bufs=6)
+            window = y_tiles[c % Y_TILES][:].indirect(pos3_sb[:, j0 // GROUP : j1 // GROUP])
+            nc.vector.tensor_tensor(results[c, j0][:], window, scaled[c][:, j0:j1], ALU.add)
 
-        def finish(c, half):
-            res = ring.tile([P, BANK], F32, name="res", tag="res", bufs=4)
-            nc.vector.tensor_scalar_max(res[:], sums[c, half][:], columns[:, TILES + c : TILES + c + 1])
-            nc.sync.dma_start(out=out[P * c : P * (c + 1), BANK * half : BANK * (half + 1)], in_=res[:])
+        def finish(c, j0, j1):
+            nc.vector.tensor_scalar_max(results[c, j0][:], results[c, j0][:], columns[:, TILES + c : TILES + c + 1])
+            nc.sync.dma_start(out=out[P * c : P * (c + 1), j0:j1], in_=results[c, j0][:])
 
+        cuts = [(0, S)] * (TILES - 2) + [(0, S // 2, S), (0, S // 2, 3 * S // 4, S)]
+        pieces = [(c, j0, j1) for c in range(TILES) for j0, j1 in zip(cuts[c], cuts[c][1:])]
         make_y(0)
-        make_y(1)
-        for step in range(2 * TILES + 1):
-            c, half = divmod(step, 2)
-            if c < TILES:
-                add_y(c, half)
+        for step in range(len(pieces) + 1):
+            if step + 1 < TILES:
+                make_y(step + 1)
+                if step + 1 >= SCALED_ON_VECTOR:
+                    scale_h(step + 1)
+            if step < len(pieces):
+                add_y(*pieces[step])
             if step >= 1:
-                finish(*divmod(step - 1, 2))
-            if half == 1 and c + 2 < TILES:
-                make_y(c + 2)
+                finish(*pieces[step - 1])

from contextlib import ExitStack

import concourse.mybir as mybir
from concourse.masks import make_identity

K, H, T, S, M = 512, 1536, 4096, 1024, 512
FLOPS = 2 * K * H * S + 2 * H * H * M

F32 = mybir.dt.float32
BF16 = mybir.dt.bfloat16
I32 = mybir.dt.int32
U32 = mybir.dt.uint32
U16 = mybir.dt.uint16
U8 = mybir.dt.uint8
FP8X4 = mybir.dt.float8_e4m3fn_x4
FP4X4 = mybir.dt.float4_e2m1fn_x4
ACT = mybir.ActivationFunctionType
ALU = mybir.AluOpType

P = 128
PACK = 4
BANK = 512
GROUP = 16
QUADRANT = 32
TILES = H // P
PASSES = H // (P * PACK)
Y_WINDOW = S + 32
Y_TILES = 3
W1_CHUNKS = (128, 128, 256, 512, 512)
W1_ON_SCALAR = 3
W1_ROUND_STEP = {1: 3, 4: 4}
SCALED_ON_VECTOR = 3

ALL_BLOCKS = ((0, 4),)
BLOCK_PAIRS = ((0, 2), (2, 4))
SHRINKING_BLOCKS = ((0, 2), (2, 3), (3, 4))


def tile_list_pearl_strand_lustre_kernel(tc, tab_words, tab_scales, offs, pos1, pos2, pos3, w1, w2_words, w2_scales, gain, low, out):
    nc = tc.nc
    with ExitStack() as ctx:
        keep = ctx.enter_context(tc.tile_pool(name="keep", bufs=1))
        ring = ctx.enter_context(tc.tile_pool(name="ring", bufs=2))
        psum = ctx.enter_context(tc.psum_pool(name="psum", bufs=1))

        offs_sb = keep.tile([P, S // GROUP], U16, name="offs_sb")
        pos1_sb = keep.tile([P, M // GROUP], U16, name="pos1_sb")
        pos2_sb = keep.tile([P, M // GROUP], U16, name="pos2_sb")
        pos3_sb = keep.tile([P, S // GROUP], U16, name="pos3_sb")
        table_words = keep.tile([P, T], I32, name="table_words", align_bytes=64)
        table_scales = keep.tile([P, T], U8, name="table_scales", align_bytes=64)
        w2_scale_sb = keep.tile([P, PASSES, H], U8, name="w2_scale_sb", align_bytes=64)
        identity = keep.tile([P, P], F32, name="identity")
        vector_rows = keep.tile([P, P], F32, name="vector_rows")
        y_tiles = [keep.tile([P, Y_WINDOW], F32, name=f"y_tile{i}") for i in range(Y_TILES)]

        nc.vector.memset(table_scales[:].bitcast(I32), 0)
        nc.vector.memset(w2_scale_sb[:].rearrange("p a n -> p (a n)").bitcast(I32), 0)
        nc.vector.memset(vector_rows[:], 0.0)
        for y_tile in y_tiles:
            nc.vector.memset(y_tile[:, M:], 0.0)
        make_identity(nc, identity[:])

        w1_starts = [sum(W1_CHUNKS[:i]) for i in range(len(W1_CHUNKS))]
        w1_raw = [keep.tile([P, PACK, width], F32, name=f"w1_raw{i}") for i, width in enumerate(W1_CHUNKS)]
        w1_by_partition = w1.rearrange("(p t) r -> p t r", t=PACK)

        def load_w1(i):
            nc.sync.dma_start(out=w1_raw[i][:], in_=w1_by_partition[:, :, w1_starts[i] : w1_starts[i] + W1_CHUNKS[i]])

        nc.sync.dma_start(offs_sb[:], offs)
        load_w1(0)
        table_in_hbm = tab_words[0].rearrange("p t i -> p (t i)").bitcast(I32)
        for first_column in (0, T // 2):
            cols = slice(first_column, first_column + T // 2)
            nc.sync.dma_start(out=table_words[:, cols], in_=table_in_hbm[:, cols])
        for q in range(P // QUADRANT):
            nc.scalar.dma_start(
                out=table_scales[QUADRANT * q : QUADRANT * q + PACK, :].bitcast(I32),
                in_=tab_scales[0, PACK * q : PACK * (q + 1), :].bitcast(I32),
            )
        load_w1(1)
        nc.sync.dma_start(pos1_sb[:], pos1)
        nc.sync.dma_start(pos2_sb[:], pos2)
        for i in range(2, len(W1_CHUNKS)):
            load_w1(i)
        w2_sb = [keep.tile([P, 2 * H], U8, name=f"w2_sb{a}", align_bytes=64) for a in range(PASSES)]
        for a in range(PASSES):
            nc.sync.dma_start(out=w2_sb[a][:].bitcast(I32), in_=w2_words[a].bitcast(I32))
        for q in range(P // QUADRANT):
            nc.sync.dma_start(
                out=w2_scale_sb[QUADRANT * q : QUADRANT * q + PACK, :, :].bitcast(I32),
                in_=w2_scales[:, PACK * q : PACK * (q + 1), :].rearrange("a s n -> s a n").bitcast(I32),
            )
        nc.sync.dma_start(pos3_sb[:], pos3)
        nc.sync.dma_start(out=vector_rows[0:TILES, :], in_=gain.rearrange("(c i) -> c i", i=P))
        nc.sync.dma_start(out=vector_rows[TILES : 2 * TILES, :], in_=low.rearrange("(c i) -> c i", i=P))

        w1_codes = [keep.tile([P, width], U32, name=f"w1_codes{i}", align_bytes=64) for i, width in enumerate(W1_CHUNKS)]
        w1_scales = [keep.tile([P, width], U8, name=f"w1_scales{i}", align_bytes=64) for i, width in enumerate(W1_CHUNKS)]
        w1_bf = [keep.tile([P, width, PACK], BF16, name=f"w1_bf{i}", align_bytes=64) for i, width in enumerate(W1_CHUNKS)]

        def round_w1(i):
            dst = w1_bf[i][:].rearrange("p (r e) t -> p r t e", e=4)
            src = w1_raw[i][:].rearrange("p t (r e) -> p r t e", e=4)
            if i < W1_ON_SCALAR:
                nc.scalar.copy(out=dst, in_=src)
            else:
                nc.vector.tensor_copy(out=dst, in_=src)

        def quantize_w1(i):
            nc.vector.quantize_mx(
                out=w1_codes[i][:].bitcast(FP8X4), scales=w1_scales[i][:], in_=w1_bf[i][:].rearrange("p r t -> p (r t)")
            )

        v_scales = keep.tile([P, S], U8, name="v_scales", align_bytes=64)
        v_words = [keep.tile([P, BANK], I32, name=f"v_words{i}", align_bytes=64) for i in range(S // BANK)]
        round_w1(0)
        quantize_w1(0)
        nc.vector.tensor_copy(v_scales[:], table_scales[:].indirect(offs_sb[:]))
        for i, j0 in enumerate(range(0, S, BANK)):
            nc.vector.tensor_copy(
                v_words[i][:].bitcast(U32),
                table_words[:].bitcast(U32).indirect(offs_sb[:, j0 // GROUP : (j0 + BANK) // GROUP]),
            )
        for i in range(1, W1_ON_SCALAR):
            round_w1(i)
            quantize_w1(i)

        h_tiles = [keep.tile([P, S], F32, name=f"h_tile{c}") for c in range(TILES)]

        def make_h(c):
            chunk = max(i for i, start in enumerate(w1_starts) if start <= P * c)
            cols = slice(P * c - w1_starts[chunk], P * (c + 1) - w1_starts[chunk])
            for i, j0 in enumerate(range(0, S, BANK)):
                acc = psum.tile([P, BANK], F32, name="acc", tag="acc", bufs=3)
                nc.tensor.matmul_mx(
                    out=acc[:],
                    lhsT=w1_codes[chunk][:, cols].bitcast(FP8X4),
                    lhsT_scale=w1_scales[chunk][:, cols],
                    rhs=v_words[i][:].bitcast(FP8X4),
                    rhs_scale=v_scales[:, j0 : j0 + BANK],
                    start=True,
                    stop=True,
                )
                nc.scalar.copy(out=h_tiles[c][:, j0 : j0 + BANK], in_=acc[:])

        magnitudes = {}

        def pick_h(c):
            picked = ring.tile([P, 2, M], F32, name="picked", tag="picked", bufs=3)
            magnitudes[c] = ring.tile([P, 2, M], F32, name="magnitudes", tag="magnitudes", bufs=3)
            for b0, b1 in SHRINKING_BLOCKS if c == TILES - 1 else ALL_BLOCKS:
                cols = slice(P * b0, P * b1)
                for which, pos_sb in enumerate((pos1_sb, pos2_sb)):
                    offsets = pos_sb[:, P * b0 // GROUP : P * b1 // GROUP]
                    nc.vector.tensor_copy(picked[:, which, cols], h_tiles[c][:].indirect(offsets))
                nc.scalar.activation(out=magnitudes[c][:, :, cols], in_=picked[:, :, cols], func=ACT.Abs)

        x_rows = {}

        def sum_x(c):
            a, q = divmod(c, PACK)
            for b0, b1 in BLOCK_PAIRS if a == PASSES - 1 else ALL_BLOCKS:
                if q == 0:
                    x_rows[a, b0] = ring.tile([P, b1 - b0, 2, P, 2], BF16, name="x_rows", tag=f"x_rows{b1 - b0}", bufs=2)
                summed = psum.tile([P, b1 - b0, P], F32, name="summed", tag="summed", bufs=3)
                for b in range(b0, b1):
                    for which in range(2):
                        nc.tensor.matmul(
                            summed[:, b - b0, :],
                            magnitudes[c][:, which, P * b : P * (b + 1)],
                            identity[:],
                            start=(which == 0),
                            stop=(which == 1),
                            is_transpose=True,
                        )
                nc.scalar.copy(
                    out=x_rows[a, b0][:, :, :, QUADRANT * q : QUADRANT * (q + 1), :],
                    in_=summed[:].rearrange("m b (p u e) -> m b u p e", u=2, e=2),
                )

        x_turned, x_bf = {}, {}
        x_codes = [keep.tile([P, M], U32, name=f"x_codes{a}", align_bytes=64) for a in range(PASSES)]
        x_scales = [keep.tile([P, M], U8, name=f"x_scales{a}", align_bytes=64) for a in range(PASSES)]

        def turn_x(a, b0, b1):
            first_block = b0 if a == PASSES - 1 else 0
            words = x_rows[a, first_block][:].rearrange("m b u p e -> m b u (p e)").bitcast(F32)
            x_turned[a, b0] = psum.tile([P, b1 - b0, 2, P], F32, name="turned", tag="turned", bufs=2)
            for b in range(b0, b1):
                for u in range(2):
                    nc.tensor.transpose(x_turned[a, b0][:, b - b0, u, :], words[:, b - first_block, u, :], identity[:])

        def weave_x(a, b0, b1):
            x_bf[a, b0] = ring.tile([P, (b1 - b0) * P * PACK], BF16, name="x_bf", tag="staged", bufs=2, align_bytes=64)
            dst = x_bf[a, b0][:].bitcast(F32).rearrange("p (b m u) -> p b m u", m=P, u=2)
            src = x_turned[a, b0][:].rearrange("p b u m -> p b m u")
            if a == PASSES - 1 and b0 > 0:
                nc.vector.tensor_copy(out=dst, in_=src)
            else:
                nc.scalar.copy(out=dst, in_=src)

        def quantize_x(a, b0, b1):
            cols = slice(P * b0, P * b1)
            nc.vector.quantize_mx(out=x_codes[a][:, cols].bitcast(FP8X4), scales=x_scales[a][:, cols], in_=x_bf[a, b0][:])

        turn_at = {PACK * a + PACK + 1 + i: (a, *pair) for a in range(PASSES - 1) for i, pair in enumerate(BLOCK_PAIRS)}
        make_h(0)
        for c in range(TILES):
            if c + 1 < TILES:
                make_h(c + 1)
            if c in turn_at:
                turn_x(*turn_at[c])
            if c >= 1:
                sum_x(c - 1)
            pick_h(c)
            if c in turn_at:
                weave_x(*turn_at[c])
            if c in W1_ROUND_STEP:
                round_w1(W1_ROUND_STEP[c])
            if c - 1 in turn_at:
                quantize_x(*turn_at[c - 1])
            if c - 1 in W1_ROUND_STEP:
                quantize_w1(W1_ROUND_STEP[c - 1])
        sum_x(TILES - 1)

        columns = keep.tile([P, 2 * TILES], F32, name="columns")
        vector_columns = psum.tile([P, P], F32, name="vector_columns", tag="summed", bufs=3)
        nc.tensor.transpose(vector_columns[:], vector_rows[:], identity[:])
        nc.vector.tensor_copy(out=columns[:], in_=vector_columns[:, 0 : 2 * TILES])
        scaled = {}
        for c in range(SCALED_ON_VECTOR):
            nc.vector.tensor_scalar_mul(h_tiles[c][:], h_tiles[c][:], columns[:, c : c + 1])
            scaled[c] = h_tiles[c]

        for b0, b1 in BLOCK_PAIRS:
            turn_x(PASSES - 1, b0, b1)
            weave_x(PASSES - 1, b0, b1)
        for b0, b1 in BLOCK_PAIRS:
            quantize_x(PASSES - 1, b0, b1)

        def make_y(c):
            acc = psum.tile([P, BANK], F32, name="acc", tag="acc", bufs=3)
            for a in range(PASSES):
                nc.tensor.matmul_mx(
                    out=acc[:],
                    lhsT=w2_sb[a][:, 2 * P * c : 2 * P * (c + 1)].bitcast(FP4X4),
                    lhsT_scale=w2_scale_sb[:, a, P * c : P * (c + 1)],
                    rhs=x_codes[a][:].bitcast(FP8X4),
                    rhs_scale=x_scales[a][:],
                    start=(a == 0),
                    stop=(a == PASSES - 1),
                )
            nc.scalar.copy(out=y_tiles[c % Y_TILES][:, 0:M], in_=acc[:])

        def scale_h(c):
            scaled[c] = ring.tile([P, S], F32, name="scaled", tag="staged", bufs=2, align_bytes=64)
            nc.scalar.activation(out=scaled[c][:], in_=h_tiles[c][:], func=ACT.Copy, scale=columns[:, c : c + 1])

        results = {}

        def add_y(c, j0, j1):
            results[c, j0] = ring.tile([P, j1 - j0], F32, name="results", tag="results", bufs=6)
            window = y_tiles[c % Y_TILES][:].indirect(pos3_sb[:, j0 // GROUP : j1 // GROUP])
            nc.vector.tensor_tensor(results[c, j0][:], window, scaled[c][:, j0:j1], ALU.add)

        def finish(c, j0, j1):
            nc.vector.tensor_scalar_max(results[c, j0][:], results[c, j0][:], columns[:, TILES + c : TILES + c + 1])
            nc.sync.dma_start(out=out[P * c : P * (c + 1), j0:j1], in_=results[c, j0][:])

        cuts = [(0, S)] * (TILES - 2) + [(0, S // 2, S), (0, S // 2, 3 * S // 4, S)]
        pieces = [(c, j0, j1) for c in range(TILES) for j0, j1 in zip(cuts[c], cuts[c][1:])]
        make_y(0)
        for step in range(len(pieces) + 1):
            if step + 1 < TILES:
                make_y(step + 1)
                if step + 1 >= SCALED_ON_VECTOR:
                    scale_h(step + 1)
            if step < len(pieces):
                add_y(*pieces[step])
            if step >= 1:
                finish(*pieces[step - 1])
